import numpy as np
import ml_dtypes


def mxq(x, axis, fmt="e4m3"):
    dtype, down = {"e4m3": (ml_dtypes.float8_e4m3fn, 7), "e5m2": (ml_dtypes.float8_e5m2, 14)}[fmt]
    v = np.moveaxis(np.asarray(x, np.float32).astype(ml_dtypes.bfloat16).astype(np.float64), axis, -1)
    blocks = v.reshape(v.shape[:-1] + (-1, 32))
    amax = np.abs(blocks).max(-1, keepdims=True)
    byte = np.maximum(np.where(amax > 0, np.frexp(amax)[1] - 1 + 127, 0) - down, 1)
    scale = np.exp2(byte - 127.0)
    codes = (blocks / scale).astype(np.float32).astype(dtype).astype(np.float64)
    return np.moveaxis((codes * scale).reshape(v.shape), -1, axis)


WIDE = False


def mx_kscale(k):
    if not WIDE:
        return np.ones(k)
    levels = np.array([10, -10, 5, -5, 0])
    if k % 512:
        return np.exp2(np.random.permutation(np.resize(levels, k // 32))).repeat(32)
    a = np.empty((k // 512, 16))
    for p in range(k // 512):
        a[p, :8] = np.random.permutation(np.resize(levels, 8))
        for g in range(8):
            far = levels[np.abs(levels - a[p, g]) >= 10]
            a[p, g + 8] = far[np.random.randint(len(far))]
    return np.exp2(a.ravel()).repeat(32)


BF16 = ml_dtypes.bfloat16


def bf(x):
    return np.asarray(x, np.float32).astype(BF16)


def f64(x):
    return np.asarray(x).astype(np.float64)


E2M1 = np.array([0.0, 0.5, 1.0, 1.5, 2.0, 3.0, 4.0, 6.0, -0.0, -0.5, -1.0, -1.5, -2.0, -3.0, -4.0, -6.0])


def pack_weight(w, fmt):
    k, n = w.shape
    w = f64(bf(w)).reshape(k // 32, 32, n)
    amax = np.abs(w).max(1)
    if fmt == "e4m3":
        byte = np.frexp(amax)[1] - 1 + 127 - 7
    else:
        mant, ex = np.frexp(amax / 6.0)
        byte = np.where(mant > 0.5, ex, ex - 1) + 127
    byte = np.clip(np.where(amax > 0, byte, 1), 1, 254)
    scaled = (w * np.exp2(127.0 - byte)[:, None, :]).reshape(k, n).astype(np.float32)
    by_word = np.ascontiguousarray(scaled.reshape(k // 512, 128, 4, n).transpose(0, 1, 3, 2))
    if fmt == "e4m3":
        words = by_word.astype(ml_dtypes.float8_e4m3fn).view(np.uint8)
    else:
        c = by_word.astype(ml_dtypes.float4_e2m1fn).view(np.uint8) & 0xF
        words = c[..., 0::2] | (c[..., 1::2] << 4)
    return np.ascontiguousarray(words), np.ascontiguousarray(byte.astype(np.uint8).reshape(k // 512, 16, n))


def unpack_weight(words, scales, fmt):
    g, p, n, _ = words.shape
    if fmt == "e4m3":
        vals = np.ascontiguousarray(words).view(ml_dtypes.float8_e4m3fn).astype(np.float64)
    else:
        nib = np.empty((g, p, n, 4), np.uint8)
        nib[..., 0::2] = words & 0xF
        nib[..., 1::2] = words >> 4
        vals = E2M1[nib]
    vals = vals * np.repeat(np.exp2(scales.astype(np.float64) - 127.0), 8, axis=1)[..., None]
    return vals.transpose(0, 1, 3, 2).reshape(g * 512, n)
def pack4(w):
    words, scales = pack_weight(w, "e2m1")
    return words.reshape(words.shape[0], 128, -1), scales


def unpack4(words, scales):
    return unpack_weight(words.reshape(words.shape[0], 128, -1, 2), scales, "e2m1")


G, U, K, R, P = 4, 1024, 1024, 512, 512


def setup_inputs():
    s = mx_kscale(G * K).reshape(G, K)
    t = mx_kscale(G * R).reshape(G, R)
    stats = np.random.standard_normal((G, U, K)) * s[:, None, :]
    a = np.random.standard_normal((G, K, R)) / np.sqrt(K) / s[:, :, None] * t[:, None, :]
    q = np.random.standard_normal((G, R, P)) / np.sqrt(R) / t[:, :, None]
    a_words, a_scales = pack4(a.reshape(G * K, R))
    q_words, q_scales = pack4(q.reshape(G * R, P))
    return {"stats": bf(stats),
            "occ": bf(np.random.uniform(0.25, 2.5, (G, U))),
            "lam": bf(np.random.uniform(0.25, 1.5, (G, R))),
            "a_words": a_words, "a_scales": a_scales,
            "q_words": q_words, "q_scales": q_scales}


def reference(stats, occ, lam, a_words, a_scales, q_words, q_scales):
    a = unpack4(a_words, a_scales).reshape(G, K, R)
    q = unpack4(q_words, q_scales).reshape(G, R, P)
    h = mxq(f64(stats), 2, "e4m3") @ a
    precision = 1.0 + f64(occ)[:, :, None] * f64(lam)[:, None, :]
    y = h / precision
    return mxq(y, 2, "e4m3") @ q

@@ -1,0 +1,343 @@
+from contextlib import ExitStack
+
+import concourse.mybir as mybir
+from concourse.masks import make_identity
+
+G, U, K, R, P = 4, 1024, 1024, 512, 512
+FLOPS = 2 * G * U * K * R + 2 * G * U * R * P
+
+F32 = mybir.dt.float32
+BF16 = mybir.dt.bfloat16
+U32 = mybir.dt.uint32
+I32 = mybir.dt.int32
+U8 = mybir.dt.uint8
+E4M3 = mybir.dt.float8_e4m3fn_x4
+E2M1 = mybir.dt.float4_e2m1fn_x4
+ACT = mybir.ActivationFunctionType
+ALU = mybir.AluOpType
+
+J = 8
+STEPS = [[1], [1], [2]] + [[2, 2]] * 6 + [[2], [1], [1]]
+
+
+def tile_grouped_ivector_extraction_s14_kernel(
+    tc, stats, occ, lam, a_words, a_scales, q_words, q_scales, out
+):
+    nc = tc.nc
+    with ExitStack() as ctx:
+        ctx.enter_context(tc.manual_schedule())
+        keep = ctx.enter_context(tc.tile_pool(name="keep", bufs=1))
+        work = ctx.enter_context(tc.tile_pool(name="work", bufs=3))
+        trp = ctx.enter_context(tc.psum_pool(name="trp", bufs=4))
+        hp = ctx.enter_context(tc.psum_pool(name="hp", bufs=2))
+        op = ctx.enter_context(tc.psum_pool(name="op", bufs=2))
+
+        units = []
+        steps = []
+        idx = 0
+        for sizes in STEPS:
+            row = []
+            for n in sizes:
+                units.append((idx // J, idx % J, n))
+                row.append(len(units) - 1)
+                idx += n
+            steps.append(row)
+
+        occ_sb = keep.tile([128, G, J], BF16, name="occ_sb", align_bytes=64)
+        lam_sb = keep.tile([128, G, 4], BF16, name="lam_sb", align_bytes=64)
+        nc.scalar.dma_start(out=occ_sb[:], in_=occ.rearrange("c (p j) -> p c j", j=J))
+        nc.scalar.dma_start(out=lam_sb[:], in_=lam.rearrange("c (p t) -> p c t", t=4))
+
+        one = keep.tile([128, 1], F32, name="one")
+        warm = keep.tile([128, 2], F32, name="warm")
+        nc.vector.memset(one[:], 1.0)
+        nc.scalar.activation(out=warm[:, 0:1], in_=one[:], func=ACT.Ln)
+
+        ident = keep.tile([128, 128], F32, name="ident")
+        make_identity(nc, ident[:])
+
+        aw = []
+        ap = []
+        for c in range(G):
+            aw.append(keep.tile([128, 2, 1024], U8, name="aw%d" % c, align_bytes=64))
+            ap.append(keep.tile([128, 2, 4, 256], U8, name="ap%d" % c, align_bytes=64))
+        as0 = keep.tile([128, 2, 512], U8, name="as0", align_bytes=64)
+        as1 = keep.tile([128, 6, 512], U8, name="as1", align_bytes=64)
+        qs = keep.tile([128, 4, 512], U8, name="qs", align_bytes=64)
+        nc.vector.memset(as0[:].rearrange("p g n -> p (g n)").bitcast(I32), 0)
+        nc.gpsimd.memset(qs[:].rearrange("p g n -> p (g n)").bitcast(I32), 0)
+        nc.gpsimd.memset(as1[:].rearrange("p g n -> p (g n)").bitcast(I32), 0)
+        asp = []
+        for c in range(G):
+            asp.append(keep.tile([128, 2, 4, 128], U8, name="asp%d" % c, align_bytes=64))
+        qw = []
+        for c in range(G):
+            qw.append(keep.tile([128, 1024], U8, name="qw%d" % c, align_bytes=64))
+
+        def load_a(c):
+            nc.sync.dma_start(
+                out=aw[c][:].bitcast(I32),
+                in_=a_words[2 * c : 2 * c + 2].rearrange("g p n -> p g n").bitcast(I32),
+            )
+
+        def load_q(c):
+            nc.sync.dma_start(out=qw[c][:].bitcast(I32), in_=q_words[c].bitcast(I32))
+
+        def load_scales(eng, dst, src):
+            for quad in range(4):
+                eng.dma_start(
+                    out=dst[32 * quad : 32 * quad + 4].bitcast(I32),
+                    in_=src[:, 4 * quad : 4 * quad + 4, :].rearrange("g r n -> r g n").bitcast(I32),
+                )
+
+        x_sb = {}
+
+        def load_x(u):
+            c, j0, n = units[u]
+            x_sb[u] = keep.tile([128, n, K], BF16, name="x%d" % u, align_bytes=64)
+            nc.sync.dma_start(
+                out=x_sb[u][:],
+                in_=stats[c].rearrange("(p j) k -> p j k", j=J)[:, j0 : j0 + n, :],
+            )
+
+        def perm_words(eng, c, g, t0, t1):
+            eng.tensor_copy(
+                out=ap[c][:, g, t0:t1, :].rearrange("p t (m b) -> p t m b", b=2),
+                in_=aw[c][:, g, :].rearrange("p (m t b) -> p t m b", t=4, b=2)[:, t0:t1],
+            )
+
+        def perm_scales(eng, c, g):
+            src = as0[:, g, :] if c == 0 else as1[:, 2 * (c - 1) + g, :]
+            eng.tensor_copy(
+                out=asp[c][:, g, :, :],
+                in_=src.rearrange("p (m t) -> p t m", t=4),
+            )
+
+        load_scales(nc.scalar, as0, a_scales[0:2])
+        load_a(0)
+        load_x(0)
+        load_x(1)
+        load_x(2)
+        load_scales(nc.sync, qs, q_scales)
+        load_q(0)
+        load_x(3)
+        load_scales(nc.sync, as1, a_scales[2:8])
+        load_x(4)
+        load_a(1)
+
+        lnocc = keep.tile([128, G * J], F32, name="lnocc")
+        lnlam = keep.tile([128, G * 4], F32, name="lnlam")
+        nlam = keep.tile([128, G * 4], F32, name="nlam")
+        nc.scalar.activation(out=lnocc[:], in_=occ_sb[:].rearrange("p c j -> p (c j)"), func=ACT.Ln)
+        nc.scalar.activation(out=lnlam[:], in_=lam_sb[:].rearrange("p c t -> p (c t)"), func=ACT.Ln)
+        nc.scalar.activation(out=warm[:, 1:2], in_=one[:], func=ACT.Sigmoid)
+        nc.vector.tensor_scalar(out=nlam[:], in0=lnlam[:], scalar1=-1.0, scalar2=None, op0=ALU.mult)
+
+        lnb = keep.tile([128, G * J, 128], F32, name="lnb")
+        for b in range(8):
+            bank = trp.tile([128, 4, 128], F32, name="tr")
+            for q in range(4):
+                i = 4 * b + q
+                nc.tensor.transpose(bank[:, q, :], lnocc[:, i : i + 1].to_broadcast([128, 128]), ident[:])
+            if b % 2 == 0:
+                nc.scalar.copy(out=lnb[:, 4 * b : 4 * b + 4, :], in_=bank[:])
+            else:
+                nc.vector.tensor_copy(out=lnb[:, 4 * b : 4 * b + 4, :], in_=bank[:])
+
+        for g in range(2):
+            perm_words(nc.vector, 0, g, 0, 4)
+        for g in range(2):
+            perm_scales(nc.vector, 0, g)
+
+        sig = {}
+
+        def sigmoid(c, t, j0, n):
+            if c not in sig:
+                sig[c] = work.tile([128, 4, J, 128], F32, name="sig", bufs=2)
+            nc.scalar.activation(
+                out=sig[c][:, t, j0 : j0 + n, :],
+                in_=lnb[:, J * c + j0 : J * c + j0 + n, :],
+                func=ACT.Sigmoid,
+                scale=-1.0,
+                bias=nlam[:, 4 * c + t : 4 * c + t + 1],
+            )
+
+        banks = {}
+        xg = {}
+        xc = {}
+        xs = {}
+        hb = {}
+        yg = {}
+        yc = {}
+        ys = {}
+        ob = {}
+
+        def transposes(u, i):
+            bank = trp.tile([128, 2, 2, 128], F32, name="tr")
+            words = x_sb[u][:, i, :].bitcast(F32)
+            for g in range(2):
+                for w in range(2):
+                    nc.tensor.transpose(bank[:, g, w, :], words[:, 256 * g + w : 256 * (g + 1) : 2], ident[:])
+            banks[(u, i)] = bank
+
+        def tout(u, i, eng):
+            n = units[u][2]
+            if u not in xg:
+                xg[u] = work.tile([128, n, 2, 128, 4], BF16, name="xg%d" % n, align_bytes=64, bufs=4 if n == 2 else 2)
+            dst = xg[u][:, i, :, :, :].bitcast(F32)
+            src = banks[(u, i)][:].rearrange("p g w r -> p g r w")
+            if eng == "s":
+                nc.scalar.copy(out=dst, in_=src)
+            else:
+                nc.vector.tensor_copy(out=dst, in_=src)
+
+        def qx(u):
+            n = units[u][2]
+            xc[u] = work.tile([128, n, 2, 128], U32, name="xc%d" % n, align_bytes=64, bufs=6 if n == 2 else 4)
+            xs[u] = work.tile([128, n, 2, 128], U8, name="xs%d" % n, align_bytes=64, bufs=6 if n == 2 else 4)
+            nc.vector.quantize_mx(
+                out=xc[u][:].rearrange("p i g r -> p (i g r)").bitcast(E4M3),
+                scales=xs[u][:].rearrange("p i g r -> p (i g r)"),
+                in_=xg[u][:].rearrange("p i g r k -> p (i g r k)"),
+            )
+
+        def mm1(u, i):
+            c = units[u][0]
+            h = hp.tile([128, 4, 128], F32, name="h")
+            for t in range(4):
+                for g in range(2):
+                    nc.tensor.matmul_mx(
+                        out=h[:, t, :],
+                        lhsT=ap[c][:, g, t, :].bitcast(E2M1),
+                        lhsT_scale=asp[c][:, g, t, :],
+                        rhs=xc[u][:, i, g, :].bitcast(E4M3),
+                        rhs_scale=xs[u][:, i, g, :],
+                        start=(g == 0),
+                        stop=(g == 1),
+                    )
+            hb[(u, i)] = h
+
+        def mult(u, i):
+            c, j0, n = units[u]
+            if u not in yg:
+                yg[u] = work.tile([128, n, 128, 4], BF16, name="yg%d" % n, align_bytes=64, bufs=4 if n == 2 else 2)
+            nc.vector.tensor_tensor(
+                out=yg[u][:, i, :, :],
+                in0=hb[(u, i)][:].rearrange("p t n -> p n t"),
+                in1=sig[c][:, :, j0 + i, :].rearrange("p t n -> p n t"),
+                op=ALU.mult,
+            )
+
+        def qy(u):
+            n = units[u][2]
+            yc[u] = work.tile([128, n, 128], U32, name="yc%d" % n, align_bytes=64, bufs=4)
+            ys[u] = work.tile([128, n, 128], U8, name="ys%d" % n, align_bytes=64, bufs=4)
+            nc.vector.quantize_mx(
+                out=yc[u][:].rearrange("p i n -> p (i n)").bitcast(E4M3),
+                scales=ys[u][:].rearrange("p i n -> p (i n)"),
+                in_=yg[u][:].rearrange("p i n k -> p (i n k)"),
+            )
+
+        def mm2(u, i):
+            c = units[u][0]
+            o = op.tile([128, 512], F32, name="o")
+            nc.tensor.matmul_mx(
+                out=o[:],
+                lhsT=yc[u][:, i, :].bitcast(E4M3),
+                lhsT_scale=ys[u][:, i, :],
+                rhs=qw[c][:].bitcast(E2M1),
+                rhs_scale=qs[:, c, :],
+                start=True,
+                stop=True,
+            )
+            ob[(u, i)] = o
+
+        o_sb = {}
+
+        def outcopy(u, i, eng):
+            c, j0, n = units[u]
+            if u not in o_sb:
+                o_sb[u] = work.tile([128, n, 512], F32, name="ot%d" % n, bufs=4)
+            if eng == "s":
+                nc.scalar.copy(out=o_sb[u][:, i, :], in_=ob[(u, i)][:])
+            else:
+                nc.vector.tensor_copy(out=o_sb[u][:, i, :], in_=ob[(u, i)][:])
+            if i == n - 1:
+                nc.sync.dma_start(
+                    out=out[c].rearrange("(p j) n -> p j n", j=J)[:, j0 : j0 + n, :],
+                    in_=o_sb[u][:],
+                )
+
+        sig_work = {}
+        first = {}
+        for s, row in enumerate(steps):
+            for u in row:
+                first.setdefault(units[u][0], s)
+        for c in range(1, G):
+            for t in range(4):
+                sig_work.setdefault(first[c] - 1 + t // 2, []).append((c, t, 0, J))
+        for t in range(4):
+            sigmoid(0, t, 0, 2)
+        sig_work.setdefault(1, []).extend([(0, t, 2, 6) for t in range(2)])
+        sig_work.setdefault(2, []).extend([(0, t, 2, 6) for t in range(2, 4)])
+
+        loaded = 5
+        perm_jobs = []
+        pending_qy = []
+        ns = len(steps)
+        for s in range(ns + 2):
+            cur = [(u, i) for u in (steps[s] if s < ns else []) for i in range(units[u][2])]
+            mid = [(u, i) for u in (steps[s - 1] if 0 <= s - 1 < ns else []) for i in range(units[u][2])]
+            last = [(u, i) for u in (steps[s - 2] if 0 <= s - 2 < ns else []) for i in range(units[u][2])]
+            while loaded < len(units) and cur and loaded <= cur[-1][0] + 5:
+                load_x(loaded)
+                c, j0, n = units[loaded]
+                if j0 == 0 and c > 0:
+                    load_q(c)
+                if j0 == 4 and c + 1 < G and c + 1 > 1:
+                    load_a(c + 1)
+                loaded += 1
+            if cur and cur[0] [1] == 0 and units[cur[0][0]][1] == 0 and units[cur[0][0]][0] + 1 < G:
+                c = units[cur[0][0]][0] + 1
+                for g in range(2):
+                    for t in range(4):
+                        perm_words(nc.gpsimd, c, g, t, t + 1)
+                    perm_scales(nc.gpsimd, c, g)
+            sw = sig_work.get(s, [])
+            for k, (u, i) in enumerate(cur):
+                transposes(u, i)
+            for k, (u, i) in enumerate(cur):
+                tout(u, i, "s" if k == 0 or (k == 2 and s % 2 == 0) else "v")
+                if k == 0 and sw:
+                    sigmoid(*sw[0])
+            for u in pending_qy:
+                qy(u)
+            pending_qy = []
+            late_qx = list(steps[s]) if s < ns else []
+            m = max(len(mid), len(last))
+            for k in range(m):
+                if k < len(mid):
+                    mm1(*mid[k])
+                    mult(*mid[k])
+                if late_qx:
+                    qx(late_qx[0])
+                    late_qx = late_qx[1:]
+                if k < len(mid):
+                    u, i = mid[k]
+                    if i == units[u][2] - 1:
+                        pending_qy.append(u)
+                    if len(pending_qy) > 1:
+                        qy(pending_qy[0])
+                        pending_qy = pending_qy[1:]
+                if k < len(last):
+                    mm2(*last[k])
+                    outcopy(last[k][0], last[k][1], "s")
+                if k == 1 or m == 1:
+                    for args in sw[1:]:
+                        sigmoid(*args)
+            for u in late_qx:
+                qx(u)
+            if s >= ns:
+                for u in pending_qy:
+                    qy(u)
+                pending_qy = []

@@ -17,7 +17,12 @@ ACT = mybir.ActivationFunctionType
 ALU = mybir.AluOpType
 
 J = 8
-STEPS = [[1], [1], [2]] + [[2, 2]] * 6 + [[2], [1], [1]]
+STEPS = [[1], [1]] + [[2]] * 14 + [[1], [1]]
+L1 = 2
+L2 = 3
+VT = (0, 1, 0, 1, 1, 0, 1, 1)
+PERM_V = False
+MMF = 3
 
 
 def tile_grouped_ivector_extraction_s14_kernel(
@@ -43,11 +48,21 @@ def tile_grouped_ivector_extraction_s14_kernel(
                 idx += n
             steps.append(row)
 
+        def load_scales(eng, dst, src):
+            for quad in range(4):
+                eng.dma_start(
+                    out=dst[32 * quad : 32 * quad + 4].bitcast(I32),
+                    in_=src[:, 4 * quad : 4 * quad + 4, :].rearrange("g r n -> r g n").bitcast(I32),
+                )
+
         occ_sb = keep.tile([128, G, J], BF16, name="occ_sb", align_bytes=64)
         lam_sb = keep.tile([128, G, 4], BF16, name="lam_sb", align_bytes=64)
         nc.scalar.dma_start(out=occ_sb[:], in_=occ.rearrange("c (p j) -> p c j", j=J))
         nc.scalar.dma_start(out=lam_sb[:], in_=lam.rearrange("c (p t) -> p c t", t=4))
 
+        as0 = keep.tile([128, 2, 512], U8, name="as0", align_bytes=64)
+        nc.vector.memset(as0[:].rearrange("p g n -> p (g n)").bitcast(I32), 0)
+        load_scales(nc.scalar, as0, a_scales[0:2])
         one = keep.tile([128, 1], F32, name="one")
         warm = keep.tile([128, 2], F32, name="warm")
         nc.vector.memset(one[:], 1.0)
@@ -61,10 +76,8 @@ def tile_grouped_ivector_extraction_s14_kernel(
         for c in range(G):
             aw.append(keep.tile([128, 2, 1024], U8, name="aw%d" % c, align_bytes=64))
             ap.append(keep.tile([128, 2, 4, 256], U8, name="ap%d" % c, align_bytes=64))
-        as0 = keep.tile([128, 2, 512], U8, name="as0", align_bytes=64)
         as1 = keep.tile([128, 6, 512], U8, name="as1", align_bytes=64)
         qs = keep.tile([128, 4, 512], U8, name="qs", align_bytes=64)
-        nc.vector.memset(as0[:].rearrange("p g n -> p (g n)").bitcast(I32), 0)
         nc.gpsimd.memset(qs[:].rearrange("p g n -> p (g n)").bitcast(I32), 0)
         nc.gpsimd.memset(as1[:].rearrange("p g n -> p (g n)").bitcast(I32), 0)
         asp = []
@@ -82,13 +95,6 @@ def tile_grouped_ivector_extraction_s14_kernel(
 
         def load_q(c):
             nc.sync.dma_start(out=qw[c][:].bitcast(I32), in_=q_words[c].bitcast(I32))
-
-        def load_scales(eng, dst, src):
-            for quad in range(4):
-                eng.dma_start(
-                    out=dst[32 * quad : 32 * quad + 4].bitcast(I32),
-                    in_=src[:, 4 * quad : 4 * quad + 4, :].rearrange("g r n -> r g n").bitcast(I32),
-                )
 
         x_sb = {}
 
@@ -113,7 +119,6 @@ def tile_grouped_ivector_extraction_s14_kernel(
                 in_=src.rearrange("p (m t) -> p t m", t=4),
             )
 
-        load_scales(nc.scalar, as0, a_scales[0:2])
         load_a(0)
         load_x(0)
         load_x(1)
@@ -134,19 +139,20 @@ def tile_grouped_ivector_extraction_s14_kernel(
         nc.vector.tensor_scalar(out=nlam[:], in0=lnlam[:], scalar1=-1.0, scalar2=None, op0=ALU.mult)
 
         lnb = keep.tile([128, G * J, 128], F32, name="lnb")
-        for b in range(8):
+
+        def spread(b, eng):
             bank = trp.tile([128, 4, 128], F32, name="tr")
             for q in range(4):
                 i = 4 * b + q
                 nc.tensor.transpose(bank[:, q, :], lnocc[:, i : i + 1].to_broadcast([128, 128]), ident[:])
-            if b % 2 == 0:
+            if eng == "s":
                 nc.scalar.copy(out=lnb[:, 4 * b : 4 * b + 4, :], in_=bank[:])
             else:
                 nc.vector.tensor_copy(out=lnb[:, 4 * b : 4 * b + 4, :], in_=bank[:])
 
+        spread(0, "v")
         for g in range(2):
             perm_words(nc.vector, 0, g, 0, 4)
-        for g in range(2):
             perm_scales(nc.vector, 0, g)
 
         sig = {}
@@ -269,26 +275,35 @@ def tile_grouped_ivector_extraction_s14_kernel(
                 )
 
         sig_work = {}
+        spread_work = {}
         first = {}
         for s, row in enumerate(steps):
             for u in row:
                 first.setdefault(units[u][0], s)
         for c in range(1, G):
             for t in range(4):
-                sig_work.setdefault(first[c] - 1 + t // 2, []).append((c, t, 0, J))
-        for t in range(4):
-            sigmoid(0, t, 0, 2)
-        sig_work.setdefault(1, []).extend([(0, t, 2, 6) for t in range(2)])
-        sig_work.setdefault(2, []).extend([(0, t, 2, 6) for t in range(2, 4)])
+                sig_work.setdefault(first[c] - 2 + t, []).append((c, t, 0, J))
+            spread_work.setdefault(first[c] - 4, []).append((2 * c, "s"))
+            spread_work.setdefault(first[c] - 3, []).append((2 * c + 1, "v"))
+        spread_work.setdefault(0, []).append((1, "v"))
+        sig_work.setdefault(0, []).extend([(0, t, 0, 1) for t in range(4)])
+        sig_work.setdefault(1, []).extend([(0, t, 1, 1) for t in range(4)])
+        sig_work.setdefault(2, []).extend([(0, t, 2, 2) for t in range(4)])
+        sig_work.setdefault(3, []).extend([(0, t, 4, 4) for t in range(2)])
+        sig_work.setdefault(4, []).extend([(0, t, 4, 4) for t in range(2, 4)])
+
+        def tiles_of(s):
+            if s < 0 or s >= len(steps):
+                return []
+            return [(u, i) for u in steps[s] for i in range(units[u][2])]
 
         loaded = 5
-        perm_jobs = []
-        pending_qy = []
         ns = len(steps)
-        for s in range(ns + 2):
-            cur = [(u, i) for u in (steps[s] if s < ns else []) for i in range(units[u][2])]
-            mid = [(u, i) for u in (steps[s - 1] if 0 <= s - 1 < ns else []) for i in range(units[u][2])]
-            last = [(u, i) for u in (steps[s - 2] if 0 <= s - 2 < ns else []) for i in range(units[u][2])]
+        count = 0
+        for s in range(ns + L2):
+            cur = tiles_of(s)
+            mid = tiles_of(s - L1)
+            last = tiles_of(s - L2)
             while loaded < len(units) and cur and loaded <= cur[-1][0] + 5:
                 load_x(loaded)
                 c, j0, n = units[loaded]
@@ -297,47 +312,41 @@ def tile_grouped_ivector_extraction_s14_kernel(
                 if j0 == 4 and c + 1 < G and c + 1 > 1:
                     load_a(c + 1)
                 loaded += 1
-            if cur and cur[0] [1] == 0 and units[cur[0][0]][1] == 0 and units[cur[0][0]][0] + 1 < G:
+            if cur and cur[0][1] == 0 and units[cur[0][0]][1] == 0 and units[cur[0][0]][0] + 1 < G:
                 c = units[cur[0][0]][0] + 1
                 for g in range(2):
                     for t in range(4):
-                        perm_words(nc.gpsimd, c, g, t, t + 1)
-                    perm_scales(nc.gpsimd, c, g)
-            sw = sig_work.get(s, [])
-            for k, (u, i) in enumerate(cur):
-                transposes(u, i)
-            for k, (u, i) in enumerate(cur):
-                tout(u, i, "s" if k == 0 or (k == 2 and s % 2 == 0) else "v")
-                if k == 0 and sw:
-                    sigmoid(*sw[0])
-            for u in pending_qy:
-                qy(u)
-            pending_qy = []
-            late_qx = list(steps[s]) if s < ns else []
-            m = max(len(mid), len(last))
-            for k in range(m):
-                if k < len(mid):
-                    mm1(*mid[k])
-                    mult(*mid[k])
-                if late_qx:
-                    qx(late_qx[0])
-                    late_qx = late_qx[1:]
-                if k < len(mid):
-                    u, i = mid[k]
-                    if i == units[u][2] - 1:
-                        pending_qy.append(u)
-                    if len(pending_qy) > 1:
-                        qy(pending_qy[0])
-                        pending_qy = pending_qy[1:]
-                if k < len(last):
-                    mm2(*last[k])
-                    outcopy(last[k][0], last[k][1], "s")
-                if k == 1 or m == 1:
-                    for args in sw[1:]:
-                        sigmoid(*args)
-            for u in late_qx:
+                        perm_words(nc.vector if PERM_V else nc.gpsimd, c, g, t, t + 1)
+                    perm_scales(nc.vector if PERM_V else nc.gpsimd, c, g)
+
+            def front():
+                for args in spread_work.get(s, []):
+                    spread(*args)
+                for u, i in cur:
+                    transposes(u, i)
+
+            def back():
+                for k in range(max(len(mid), len(last))):
+                    if k < len(mid):
+                        mm1(*mid[k])
+                        mult(*mid[k])
+                    if k < len(last):
+                        mm2(*last[k])
+                        outcopy(last[k][0], last[k][1], "s")
+
+            for u in (steps[s - 1] if 1 <= s <= ns else []):
                 qx(u)
-            if s >= ns:
-                for u in pending_qy:
-                    qy(u)
-                pending_qy = []
+            for u in (steps[s - L1 - 1] if 0 <= s - L1 - 1 < ns else []):
+                qy(u)
+            if s < MMF:
+                back()
+                front()
+            else:
+                front()
+            for k, (u, i) in enumerate(cur):
+                tout(u, i, "v" if VT[count % 8] else "s")
+                count += 1
+            for args in sig_work.get(s, []):
+                sigmoid(*args)
+            if s >= MMF:
+                back()

@@ -20,8 +20,7 @@ J = 8
 STEPS = [[1], [1]] + [[2]] * 14 + [[1], [1]]
 L1 = 2
 L2 = 3
-VT = (0, 1, 0, 1, 1, 0, 1, 1)
-PERM_V = False
+VT = (0, 1)
 MMF = 3
 
 
@@ -228,9 +227,9 @@ def tile_grouped_ivector_extraction_s14_kernel(
             if u not in yg:
                 yg[u] = work.tile([128, n, 128, 4], BF16, name="yg%d" % n, align_bytes=64, bufs=4 if n == 2 else 2)
             nc.vector.tensor_tensor(
-                out=yg[u][:, i, :, :],
-                in0=hb[(u, i)][:].rearrange("p t n -> p n t"),
-                in1=sig[c][:, :, j0 + i, :].rearrange("p t n -> p n t"),
+                out=yg[u][:, i, :, :].rearrange("p (b e) t -> p b t e", e=4),
+                in0=hb[(u, i)][:].rearrange("p t (b e) -> p b t e", e=4),
+                in1=sig[c][:, :, j0 + i, :].rearrange("p t (b e) -> p b t e", e=4),
                 op=ALU.mult,
             )
 
@@ -297,6 +296,11 @@ def tile_grouped_ivector_extraction_s14_kernel(
                 return []
             return [(u, i) for u in steps[s] for i in range(units[u][2])]
 
+        perm_work = {}
+        for c in range(1, G):
+            for g in range(2):
+                perm_work.setdefault(first[c] - 2 + 2 * g, []).append((perm_words, (nc.vector, c, g, 0, 4)))
+                perm_work.setdefault(first[c] - 1 + 2 * g, []).append((perm_scales, (nc.vector, c, g)))
         loaded = 5
         ns = len(steps)
         count = 0
@@ -312,12 +316,6 @@ def tile_grouped_ivector_extraction_s14_kernel(
                 if j0 == 4 and c + 1 < G and c + 1 > 1:
                     load_a(c + 1)
                 loaded += 1
-            if cur and cur[0][1] == 0 and units[cur[0][0]][1] == 0 and units[cur[0][0]][0] + 1 < G:
-                c = units[cur[0][0]][0] + 1
-                for g in range(2):
-                    for t in range(4):
-                        perm_words(nc.vector if PERM_V else nc.gpsimd, c, g, t, t + 1)
-                    perm_scales(nc.vector if PERM_V else nc.gpsimd, c, g)
 
             def front():
                 for args in spread_work.get(s, []):
@@ -344,9 +342,11 @@ def tile_grouped_ivector_extraction_s14_kernel(
             else:
                 front()
             for k, (u, i) in enumerate(cur):
-                tout(u, i, "v" if VT[count % 8] else "s")
+                tout(u, i, "v" if VT[count % 2] else "s")
                 count += 1
             for args in sig_work.get(s, []):
                 sigmoid(*args)
+            for f, args in perm_work.get(s, []):
+                f(*args)
             if s >= MMF:
                 back()

@@ -17,11 +17,10 @@ ACT = mybir.ActivationFunctionType
 ALU = mybir.AluOpType
 
 J = 8
-STEPS = [[1], [1]] + [[2]] * 14 + [[1], [1]]
+STEPS = [[1], [1]] + [[2]] * 14 + [[1, 1]]
 L1 = 2
 L2 = 3
 VT = (0, 1)
-MMF = 3
 
 
 def tile_grouped_ivector_extraction_s14_kernel(
@@ -47,8 +46,9 @@ def tile_grouped_ivector_extraction_s14_kernel(
                 idx += n
             steps.append(row)
 
-        def load_scales(eng, dst, src):
+        def load_scales(engines, dst, src):
             for quad in range(4):
+                eng = engines[quad % len(engines)]
                 eng.dma_start(
                     out=dst[32 * quad : 32 * quad + 4].bitcast(I32),
                     in_=src[:, 4 * quad : 4 * quad + 4, :].rearrange("g r n -> r g n").bitcast(I32),
@@ -61,7 +61,7 @@ def tile_grouped_ivector_extraction_s14_kernel(
 
         as0 = keep.tile([128, 2, 512], U8, name="as0", align_bytes=64)
         nc.vector.memset(as0[:].rearrange("p g n -> p (g n)").bitcast(I32), 0)
-        load_scales(nc.scalar, as0, a_scales[0:2])
+        load_scales((nc.scalar, nc.gpsimd), as0, a_scales[0:2])
         one = keep.tile([128, 1], F32, name="one")
         warm = keep.tile([128, 2], F32, name="warm")
         nc.vector.memset(one[:], 1.0)
@@ -122,12 +122,6 @@ def tile_grouped_ivector_extraction_s14_kernel(
         load_x(0)
         load_x(1)
         load_x(2)
-        load_scales(nc.sync, qs, q_scales)
-        load_q(0)
-        load_x(3)
-        load_scales(nc.sync, as1, a_scales[2:8])
-        load_x(4)
-        load_a(1)
 
         lnocc = keep.tile([128, G * J], F32, name="lnocc")
         lnlam = keep.tile([128, G * 4], F32, name="lnlam")
@@ -137,7 +131,26 @@ def tile_grouped_ivector_extraction_s14_kernel(
         nc.scalar.activation(out=warm[:, 1:2], in_=one[:], func=ACT.Sigmoid)
         nc.vector.tensor_scalar(out=nlam[:], in0=lnlam[:], scalar1=-1.0, scalar2=None, op0=ALU.mult)
 
-        lnb = keep.tile([128, G * J, 128], F32, name="lnb")
+        lnb = keep.tile([128, J, 128], F32, name="lnb")
+        lnu = keep.tile([128, G - 1, U], F32, name="lnu")
+        park = out[G - 1, U - 8 : U, :].rearrange("a b -> (a b)")
+        nc.scalar.dma_start(
+            out=park.rearrange("(c p j) -> p c j", c=G, j=J),
+            in_=lnocc[:].rearrange("p (c j) -> p c j", j=J),
+        )
+
+        load_scales((nc.gpsimd,), qs, q_scales)
+        load_scales((nc.gpsimd,), as1, a_scales[2:8])
+        load_q(0)
+        load_x(3)
+        load_x(4)
+        load_a(1)
+
+        def load_lnu(c):
+            nc.sync.dma_start(
+                out=lnu[:, c - 1, :],
+                in_=park[U * c : U * (c + 1)].partition_broadcast(128),
+            )
 
         def spread(b, eng):
             bank = trp.tile([128, 4, 128], F32, name="tr")
@@ -152,6 +165,8 @@ def tile_grouped_ivector_extraction_s14_kernel(
         spread(0, "v")
         for g in range(2):
             perm_words(nc.vector, 0, g, 0, 4)
+        spread(1, "v")
+        for g in range(2):
             perm_scales(nc.vector, 0, g)
 
         sig = {}
@@ -161,7 +176,7 @@ def tile_grouped_ivector_extraction_s14_kernel(
                 sig[c] = work.tile([128, 4, J, 128], F32, name="sig", bufs=2)
             nc.scalar.activation(
                 out=sig[c][:, t, j0 : j0 + n, :],
-                in_=lnb[:, J * c + j0 : J * c + j0 + n, :],
+                in_=lnb[:, j0 : j0 + n, :] if c == 0 else lnu[:, c - 1, :].rearrange("p (m j) -> p j m", j=J),
                 func=ACT.Sigmoid,
                 scale=-1.0,
                 bias=nlam[:, 4 * c + t : 4 * c + t + 1],
@@ -282,9 +297,6 @@ def tile_grouped_ivector_extraction_s14_kernel(
         for c in range(1, G):
             for t in range(4):
                 sig_work.setdefault(first[c] - 2 + t, []).append((c, t, 0, J))
-            spread_work.setdefault(first[c] - 4, []).append((2 * c, "s"))
-            spread_work.setdefault(first[c] - 3, []).append((2 * c + 1, "v"))
-        spread_work.setdefault(0, []).append((1, "v"))
         sig_work.setdefault(0, []).extend([(0, t, 0, 1) for t in range(4)])
         sig_work.setdefault(1, []).extend([(0, t, 1, 1) for t in range(4)])
         sig_work.setdefault(2, []).extend([(0, t, 2, 2) for t in range(4)])
@@ -301,6 +313,7 @@ def tile_grouped_ivector_extraction_s14_kernel(
             for g in range(2):
                 perm_work.setdefault(first[c] - 2 + 2 * g, []).append((perm_words, (nc.vector, c, g, 0, 4)))
                 perm_work.setdefault(first[c] - 1 + 2 * g, []).append((perm_scales, (nc.vector, c, g)))
+        load_lnu(1)
         loaded = 5
         ns = len(steps)
         count = 0
@@ -313,6 +326,8 @@ def tile_grouped_ivector_extraction_s14_kernel(
                 c, j0, n = units[loaded]
                 if j0 == 0 and c > 0:
                     load_q(c)
+                    if c + 1 < G:
+                        load_lnu(c + 1)
                 if j0 == 4 and c + 1 < G and c + 1 > 1:
                     load_a(c + 1)
                 loaded += 1
@@ -324,23 +339,22 @@ def tile_grouped_ivector_extraction_s14_kernel(
                     transposes(u, i)
 
             def back():
-                for k in range(max(len(mid), len(last))):
-                    if k < len(mid):
+                order = [(k, f) for k in range(2) for f in range(2)]
+                if s == ns + 1:
+                    order = [(k, f) for f in range(2) for k in range(2)]
+                for k, f in order:
+                    if f == 0 and k < len(mid):
                         mm1(*mid[k])
                         mult(*mid[k])
-                    if k < len(last):
+                    if f == 1 and k < len(last):
                         mm2(*last[k])
-                        outcopy(last[k][0], last[k][1], "s")
+                        outcopy(last[k][0], last[k][1], "v" if s == ns + 2 and k == 0 else "s")
 
             for u in (steps[s - 1] if 1 <= s <= ns else []):
                 qx(u)
             for u in (steps[s - L1 - 1] if 0 <= s - L1 - 1 < ns else []):
                 qy(u)
-            if s < MMF:
-                back()
-                front()
-            else:
-                front()
+            front()
             for k, (u, i) in enumerate(cur):
                 tout(u, i, "v" if VT[count % 2] else "s")
                 count += 1
@@ -348,5 +362,4 @@ def tile_grouped_ivector_extraction_s14_kernel(
                 sigmoid(*args)
             for f, args in perm_work.get(s, []):
                 f(*args)
-            if s >= MMF:
-                back()
+            back()

@@ -20,6 +20,9 @@ J = 8
 STEPS = [[1], [1]] + [[2]] * 14 + [[1, 1]]
 L1 = 2
 L2 = 3
+PL = 2
+SL = 4
+BF = 2
 VT = (0, 1)
 
 
@@ -54,21 +57,20 @@ def tile_grouped_ivector_extraction_s14_kernel(
                     in_=src[:, 4 * quad : 4 * quad + 4, :].rearrange("g r n -> r g n").bitcast(I32),
                 )
 
-        occ_sb = keep.tile([128, G, J], BF16, name="occ_sb", align_bytes=64)
+        occ_r = keep.tile([G * J, 128], BF16, name="occ_r", align_bytes=64)
         lam_sb = keep.tile([128, G, 4], BF16, name="lam_sb", align_bytes=64)
-        nc.scalar.dma_start(out=occ_sb[:], in_=occ.rearrange("c (p j) -> p c j", j=J))
+        nc.scalar.dma_start(out=occ_r[:], in_=occ.rearrange("c (b m) -> (c b) m", m=128))
         nc.scalar.dma_start(out=lam_sb[:], in_=lam.rearrange("c (p t) -> p c t", t=4))
 
+        ident = keep.tile([128, 128], F32, name="ident")
+        make_identity(nc, ident[:])
         as0 = keep.tile([128, 2, 512], U8, name="as0", align_bytes=64)
         nc.vector.memset(as0[:].rearrange("p g n -> p (g n)").bitcast(I32), 0)
-        load_scales((nc.scalar, nc.gpsimd), as0, a_scales[0:2])
         one = keep.tile([128, 1], F32, name="one")
         warm = keep.tile([128, 2], F32, name="warm")
         nc.vector.memset(one[:], 1.0)
         nc.scalar.activation(out=warm[:, 0:1], in_=one[:], func=ACT.Ln)
 
-        ident = keep.tile([128, 128], F32, name="ident")
-        make_identity(nc, ident[:])
 
         aw = []
         ap = []
@@ -102,7 +104,7 @@ def tile_grouped_ivector_extraction_s14_kernel(
             x_sb[u] = keep.tile([128, n, K], BF16, name="x%d" % u, align_bytes=64)
             nc.sync.dma_start(
                 out=x_sb[u][:],
-                in_=stats[c].rearrange("(p j) k -> p j k", j=J)[:, j0 : j0 + n, :],
+                in_=stats[c].rearrange("(j p) k -> p j k", j=J)[:, j0 : j0 + n, :],
             )
 
         def perm_words(eng, c, g, t0, t1):
@@ -120,31 +122,41 @@ def tile_grouped_ivector_extraction_s14_kernel(
 
         load_a(0)
         load_x(0)
+        load_scales((nc.sync,), as0, a_scales[0:2])
         load_x(1)
         load_x(2)
 
-        lnocc = keep.tile([128, G * J], F32, name="lnocc")
+        lnr = keep.tile([128, 128], F32, name="lnr")
+        lnc = keep.tile([128, G * J], F32, name="lnc")
+        nc.vector.memset(lnr[:], 0.0)
         lnlam = keep.tile([128, G * 4], F32, name="lnlam")
         nlam = keep.tile([128, G * 4], F32, name="nlam")
-        nc.scalar.activation(out=lnocc[:], in_=occ_sb[:].rearrange("p c j -> p (c j)"), func=ACT.Ln)
+        lnb = keep.tile([128, J, 128], F32, name="lnb")
+        lnu = keep.tile([128, G - 1, U], F32, name="lnu")
+        nc.scalar.activation(out=lnr[0 : G * J, :], in_=occ_r[:], func=ACT.Ln)
         nc.scalar.activation(out=lnlam[:], in_=lam_sb[:].rearrange("p c t -> p (c t)"), func=ACT.Ln)
         nc.scalar.activation(out=warm[:, 1:2], in_=one[:], func=ACT.Sigmoid)
         nc.vector.tensor_scalar(out=nlam[:], in0=lnlam[:], scalar1=-1.0, scalar2=None, op0=ALU.mult)
+        bank = trp.tile([128, 4, 128], F32, name="tr")
+        nc.tensor.transpose(bank[:, 0, :], lnr[:], ident[:])
+        nc.vector.tensor_copy(out=lnc[:], in_=bank[:, 0, 0 : G * J])
 
-        lnb = keep.tile([128, J, 128], F32, name="lnb")
-        lnu = keep.tile([128, G - 1, U], F32, name="lnu")
+        def spread(b):
+            bank = trp.tile([128, 4, 128], F32, name="tr")
+            for k in range(4):
+                i = 4 * b + k
+                nc.tensor.transpose(bank[:, k, :], lnc[:, i : i + 1].to_broadcast([128, 128]), ident[:])
+            nc.scalar.copy(out=lnb[:, 4 * b : 4 * b + 4, :], in_=bank[:])
+
+        spread(0)
         park = out[G - 1, U - 8 : U, :].rearrange("a b -> (a b)")
-        nc.scalar.dma_start(
-            out=park.rearrange("(c p j) -> p c j", c=G, j=J),
-            in_=lnocc[:].rearrange("p (c j) -> p c j", j=J),
-        )
-
-        load_scales((nc.gpsimd,), qs, q_scales)
-        load_scales((nc.gpsimd,), as1, a_scales[2:8])
-        load_q(0)
         load_x(3)
+        load_q(0)
+        nc.sync.dma_start(out=park.rearrange("(q p) -> q p", p=128), in_=lnr[0 : G * J, :])
+        load_scales((nc.sync,), qs, q_scales)
         load_x(4)
         load_a(1)
+        load_scales((nc.sync,), as1, a_scales[2:8])
 
         def load_lnu(c):
             nc.sync.dma_start(
@@ -152,22 +164,8 @@ def tile_grouped_ivector_extraction_s14_kernel(
                 in_=park[U * c : U * (c + 1)].partition_broadcast(128),
             )
 
-        def spread(b, eng):
-            bank = trp.tile([128, 4, 128], F32, name="tr")
-            for q in range(4):
-                i = 4 * b + q
-                nc.tensor.transpose(bank[:, q, :], lnocc[:, i : i + 1].to_broadcast([128, 128]), ident[:])
-            if eng == "s":
-                nc.scalar.copy(out=lnb[:, 4 * b : 4 * b + 4, :], in_=bank[:])
-            else:
-                nc.vector.tensor_copy(out=lnb[:, 4 * b : 4 * b + 4, :], in_=bank[:])
-
-        spread(0, "v")
         for g in range(2):
             perm_words(nc.vector, 0, g, 0, 4)
-        spread(1, "v")
-        for g in range(2):
-            perm_scales(nc.vector, 0, g)
 
         sig = {}
 
@@ -175,8 +173,8 @@ def tile_grouped_ivector_extraction_s14_kernel(
             if c not in sig:
                 sig[c] = work.tile([128, 4, J, 128], F32, name="sig", bufs=2)
             nc.scalar.activation(
-                out=sig[c][:, t, j0 : j0 + n, :],
-                in_=lnb[:, j0 : j0 + n, :] if c == 0 else lnu[:, c - 1, :].rearrange("p (m j) -> p j m", j=J),
+                out=sig[c][:, t, j0 : j0 + n, :] if c == 0 else sig[c][:, t, :, :].rearrange("p j m -> p (j m)"),
+                in_=lnb[:, j0 : j0 + n, :] if c == 0 else lnu[:, c - 1, :],
                 func=ACT.Sigmoid,
                 scale=-1.0,
                 bias=nlam[:, 4 * c + t : 4 * c + t + 1],
@@ -284,36 +282,35 @@ def tile_grouped_ivector_extraction_s14_kernel(
                 nc.vector.tensor_copy(out=o_sb[u][:, i, :], in_=ob[(u, i)][:])
             if i == n - 1:
                 nc.sync.dma_start(
-                    out=out[c].rearrange("(p j) n -> p j n", j=J)[:, j0 : j0 + n, :],
+                    out=out[c].rearrange("(j p) n -> p j n", j=J)[:, j0 : j0 + n, :],
                     in_=o_sb[u][:],
                 )
 
         sig_work = {}
-        spread_work = {}
         first = {}
+        step_of = [s for s, row in enumerate(steps) for u in row for i in range(units[u][2])]
         for s, row in enumerate(steps):
             for u in row:
                 first.setdefault(units[u][0], s)
-        for c in range(1, G):
-            for t in range(4):
-                sig_work.setdefault(first[c] - 2 + t, []).append((c, t, 0, J))
         sig_work.setdefault(0, []).extend([(0, t, 0, 1) for t in range(4)])
         sig_work.setdefault(1, []).extend([(0, t, 1, 1) for t in range(4)])
         sig_work.setdefault(2, []).extend([(0, t, 2, 2) for t in range(4)])
         sig_work.setdefault(3, []).extend([(0, t, 4, 4) for t in range(2)])
         sig_work.setdefault(4, []).extend([(0, t, 4, 4) for t in range(2, 4)])
+        for c in range(1, G):
+            for t in range(4):
+                sig_work.setdefault(step_of[min(8 * c - (2 if c == 1 else SL) + 2 * t, 31)], []).append((c, t, 0, J))
 
         def tiles_of(s):
             if s < 0 or s >= len(steps):
                 return []
             return [(u, i) for u in steps[s] for i in range(units[u][2])]
 
-        perm_work = {}
+        perm_work = {0: [(perm_scales, (nc.vector, 0, g)) for g in range(2)]}
         for c in range(1, G):
             for g in range(2):
-                perm_work.setdefault(first[c] - 2 + 2 * g, []).append((perm_words, (nc.vector, c, g, 0, 4)))
-                perm_work.setdefault(first[c] - 1 + 2 * g, []).append((perm_scales, (nc.vector, c, g)))
-        load_lnu(1)
+                perm_work.setdefault(step_of[8 * c - 2 * PL + 4 * g], []).append((perm_words, (nc.vector, c, g, 0, 4)))
+                perm_work.setdefault(step_of[8 * c - 2 * PL + 4 * g + 2], []).append((perm_scales, (nc.vector, c, g)))
         loaded = 5
         ns = len(steps)
         count = 0
@@ -323,6 +320,8 @@ def tile_grouped_ivector_extraction_s14_kernel(
             last = tiles_of(s - L2)
             while loaded < len(units) and cur and loaded <= cur[-1][0] + 5:
                 load_x(loaded)
+                if loaded == 5:
+                    load_lnu(1)
                 c, j0, n = units[loaded]
                 if j0 == 0 and c > 0:
                     load_q(c)
@@ -333,33 +332,43 @@ def tile_grouped_ivector_extraction_s14_kernel(
                 loaded += 1
 
             def front():
-                for args in spread_work.get(s, []):
-                    spread(*args)
+                if s == 2:
+                    spread(1)
                 for u, i in cur:
                     transposes(u, i)
 
             def back():
-                order = [(k, f) for k in range(2) for f in range(2)]
-                if s == ns + 1:
-                    order = [(k, f) for f in range(2) for k in range(2)]
+                order = [(k, f) for k in range(4) for f in range(2)]
+                if s == ns + L1 - 1:
+                    order = [(k, f) for f in range(2) for k in range(4)]
                 for k, f in order:
                     if f == 0 and k < len(mid):
                         mm1(*mid[k])
                         mult(*mid[k])
                     if f == 1 and k < len(last):
                         mm2(*last[k])
-                        outcopy(last[k][0], last[k][1], "v" if s == ns + 2 and k == 0 else "s")
+                        outcopy(last[k][0], last[k][1], "v" if s == ns + L2 - 1 and k == 0 else "s")
 
+            qy_units = steps[s - L1 - 1] if 0 <= s - L1 - 1 < ns else []
+            if s == ns:
+                for u in qy_units:
+                    qy(u)
             for u in (steps[s - 1] if 1 <= s <= ns else []):
                 qx(u)
-            for u in (steps[s - L1 - 1] if 0 <= s - L1 - 1 < ns else []):
-                qy(u)
-            front()
+            if s != ns:
+                for u in qy_units:
+                    qy(u)
+            if s == BF:
+                back()
+                front()
+            else:
+                front()
             for k, (u, i) in enumerate(cur):
-                tout(u, i, "v" if VT[count % 2] else "s")
+                tout(u, i, "v" if VT[count % 2] != (s < 2) else "s")
                 count += 1
             for args in sig_work.get(s, []):
                 sigmoid(*args)
             for f, args in perm_work.get(s, []):
                 f(*args)
-            back()
+            if s != BF:
+                back()

from contextlib import ExitStack

import concourse.mybir as mybir
from concourse.masks import make_identity

G, U, K, R, P = 4, 1024, 1024, 512, 512
FLOPS = 2 * G * U * K * R + 2 * G * U * R * P

F32 = mybir.dt.float32
BF16 = mybir.dt.bfloat16
U32 = mybir.dt.uint32
I32 = mybir.dt.int32
U8 = mybir.dt.uint8
E4M3 = mybir.dt.float8_e4m3fn_x4
E2M1 = mybir.dt.float4_e2m1fn_x4
ACT = mybir.ActivationFunctionType
ALU = mybir.AluOpType

J = 8
STEPS = [[1], [1]] + [[2]] * 14 + [[1, 1]]
L1 = 2
L2 = 3
PL = 2
SL = 4
BF = 2
VT = (0, 1)


def tile_grouped_ivector_extraction_s14_kernel(
    tc, stats, occ, lam, a_words, a_scales, q_words, q_scales, out
):
    nc = tc.nc
    with ExitStack() as ctx:
        ctx.enter_context(tc.manual_schedule())
        keep = ctx.enter_context(tc.tile_pool(name="keep", bufs=1))
        work = ctx.enter_context(tc.tile_pool(name="work", bufs=3))
        trp = ctx.enter_context(tc.psum_pool(name="trp", bufs=4))
        hp = ctx.enter_context(tc.psum_pool(name="hp", bufs=2))
        op = ctx.enter_context(tc.psum_pool(name="op", bufs=2))

        units = []
        steps = []
        idx = 0
        for sizes in STEPS:
            row = []
            for n in sizes:
                units.append((idx // J, idx % J, n))
                row.append(len(units) - 1)
                idx += n
            steps.append(row)

        def load_scales(engines, dst, src):
            for quad in range(4):
                eng = engines[quad % len(engines)]
                eng.dma_start(
                    out=dst[32 * quad : 32 * quad + 4].bitcast(I32),
                    in_=src[:, 4 * quad : 4 * quad + 4, :].rearrange("g r n -> r g n").bitcast(I32),
                )

        occ_r = keep.tile([G * J, 128], BF16, name="occ_r", align_bytes=64)
        lam_sb = keep.tile([128, G, 4], BF16, name="lam_sb", align_bytes=64)
        nc.scalar.dma_start(out=occ_r[:], in_=occ.rearrange("c (b m) -> (c b) m", m=128))
        nc.scalar.dma_start(out=lam_sb[:], in_=lam.rearrange("c (p t) -> p c t", t=4))

        ident = keep.tile([128, 128], F32, name="ident")
        make_identity(nc, ident[:])
        as0 = keep.tile([128, 2, 512], U8, name="as0", align_bytes=64)
        nc.vector.memset(as0[:].rearrange("p g n -> p (g n)").bitcast(I32), 0)
        one = keep.tile([128, 1], F32, name="one")
        warm = keep.tile([128, 2], F32, name="warm")
        nc.vector.memset(one[:], 1.0)
        nc.scalar.activation(out=warm[:, 0:1], in_=one[:], func=ACT.Ln)


        aw = []
        ap = []
        for c in range(G):
            aw.append(keep.tile([128, 2, 1024], U8, name="aw%d" % c, align_bytes=64))
            ap.append(keep.tile([128, 2, 4, 256], U8, name="ap%d" % c, align_bytes=64))
        as1 = keep.tile([128, 6, 512], U8, name="as1", align_bytes=64)
        qs = keep.tile([128, 4, 512], U8, name="qs", align_bytes=64)
        nc.gpsimd.memset(qs[:].rearrange("p g n -> p (g n)").bitcast(I32), 0)
        nc.gpsimd.memset(as1[:].rearrange("p g n -> p (g n)").bitcast(I32), 0)
        asp = []
        for c in range(G):
            asp.append(keep.tile([128, 2, 4, 128], U8, name="asp%d" % c, align_bytes=64))
        qw = []
        for c in range(G):
            qw.append(keep.tile([128, 1024], U8, name="qw%d" % c, align_bytes=64))

        def load_a(c):
            nc.sync.dma_start(
                out=aw[c][:].bitcast(I32),
                in_=a_words[2 * c : 2 * c + 2].rearrange("g p n -> p g n").bitcast(I32),
            )

        def load_q(c):
            nc.sync.dma_start(out=qw[c][:].bitcast(I32), in_=q_words[c].bitcast(I32))

        x_sb = {}

        def load_x(u):
            c, j0, n = units[u]
            x_sb[u] = keep.tile([128, n, K], BF16, name="x%d" % u, align_bytes=64)
            nc.sync.dma_start(
                out=x_sb[u][:],
                in_=stats[c].rearrange("(j p) k -> p j k", j=J)[:, j0 : j0 + n, :],
            )

        def perm_words(eng, c, g, t0, t1):
            eng.tensor_copy(
                out=ap[c][:, g, t0:t1, :].rearrange("p t (m b) -> p t m b", b=2),
                in_=aw[c][:, g, :].rearrange("p (m t b) -> p t m b", t=4, b=2)[:, t0:t1],
            )

        def perm_scales(eng, c, g):
            src = as0[:, g, :] if c == 0 else as1[:, 2 * (c - 1) + g, :]
            eng.tensor_copy(
                out=asp[c][:, g, :, :],
                in_=src.rearrange("p (m t) -> p t m", t=4),
            )

        load_a(0)
        load_x(0)
        load_scales((nc.sync,), as0, a_scales[0:2])
        load_x(1)
        load_x(2)

        lnr = keep.tile([128, 128], F32, name="lnr")
        lnc = keep.tile([128, G * J], F32, name="lnc")
        nc.vector.memset(lnr[:], 0.0)
        lnlam = keep.tile([128, G * 4], F32, name="lnlam")
        nlam = keep.tile([128, G * 4], F32, name="nlam")
        lnb = keep.tile([128, J, 128], F32, name="lnb")
        lnu = keep.tile([128, G - 1, U], F32, name="lnu")
        nc.scalar.activation(out=lnr[0 : G * J, :], in_=occ_r[:], func=ACT.Ln)
        nc.scalar.activation(out=lnlam[:], in_=lam_sb[:].rearrange("p c t -> p (c t)"), func=ACT.Ln)
        nc.scalar.activation(out=warm[:, 1:2], in_=one[:], func=ACT.Sigmoid)
        nc.vector.tensor_scalar(out=nlam[:], in0=lnlam[:], scalar1=-1.0, scalar2=None, op0=ALU.mult)
        bank = trp.tile([128, 4, 128], F32, name="tr")
        nc.tensor.transpose(bank[:, 0, :], lnr[:], ident[:])
        nc.vector.tensor_copy(out=lnc[:], in_=bank[:, 0, 0 : G * J])

        def spread(b):
            bank = trp.tile([128, 4, 128], F32, name="tr")
            for k in range(4):
                i = 4 * b + k
                nc.tensor.transpose(bank[:, k, :], lnc[:, i : i + 1].to_broadcast([128, 128]), ident[:])
            nc.scalar.copy(out=lnb[:, 4 * b : 4 * b + 4, :], in_=bank[:])

        spread(0)
        park = out[G - 1, U - 8 : U, :].rearrange("a b -> (a b)")
        load_x(3)
        load_q(0)
        nc.sync.dma_start(out=park.rearrange("(q p) -> q p", p=128), in_=lnr[0 : G * J, :])
        load_scales((nc.sync,), qs, q_scales)
        load_x(4)
        load_a(1)
        load_scales((nc.sync,), as1, a_scales[2:8])

        def load_lnu(c):
            nc.sync.dma_start(
                out=lnu[:, c - 1, :],
                in_=park[U * c : U * (c + 1)].partition_broadcast(128),
            )

        for g in range(2):
            perm_words(nc.vector, 0, g, 0, 4)

        sig = {}

        def sigmoid(c, t, j0, n):
            if c not in sig:
                sig[c] = work.tile([128, 4, J, 128], F32, name="sig", bufs=2)
            nc.scalar.activation(
                out=sig[c][:, t, j0 : j0 + n, :] if c == 0 else sig[c][:, t, :, :].rearrange("p j m -> p (j m)"),
                in_=lnb[:, j0 : j0 + n, :] if c == 0 else lnu[:, c - 1, :],
                func=ACT.Sigmoid,
                scale=-1.0,
                bias=nlam[:, 4 * c + t : 4 * c + t + 1],
            )

        banks = {}
        xg = {}
        xc = {}
        xs = {}
        hb = {}
        yg = {}
        yc = {}
        ys = {}
        ob = {}

        def transposes(u, i):
            bank = trp.tile([128, 2, 2, 128], F32, name="tr")
            words = x_sb[u][:, i, :].bitcast(F32)
            for g in range(2):
                for w in range(2):
                    nc.tensor.transpose(bank[:, g, w, :], words[:, 256 * g + w : 256 * (g + 1) : 2], ident[:])
            banks[(u, i)] = bank

        def tout(u, i, eng):
            n = units[u][2]
            if u not in xg:
                xg[u] = work.tile([128, n, 2, 128, 4], BF16, name="xg%d" % n, align_bytes=64, bufs=4 if n == 2 else 2)
            dst = xg[u][:, i, :, :, :].bitcast(F32)
            src = banks[(u, i)][:].rearrange("p g w r -> p g r w")
            if eng == "s":
                nc.scalar.copy(out=dst, in_=src)
            else:
                nc.vector.tensor_copy(out=dst, in_=src)

        def qx(u):
            n = units[u][2]
            xc[u] = work.tile([128, n, 2, 128], U32, name="xc%d" % n, align_bytes=64, bufs=6 if n == 2 else 4)
            xs[u] = work.tile([128, n, 2, 128], U8, name="xs%d" % n, align_bytes=64, bufs=6 if n == 2 else 4)
            nc.vector.quantize_mx(
                out=xc[u][:].rearrange("p i g r -> p (i g r)").bitcast(E4M3),
                scales=xs[u][:].rearrange("p i g r -> p (i g r)"),
                in_=xg[u][:].rearrange("p i g r k -> p (i g r k)"),
            )

        def mm1(u, i):
            c = units[u][0]
            h = hp.tile([128, 4, 128], F32, name="h")
            for t in range(4):
                for g in range(2):
                    nc.tensor.matmul_mx(
                        out=h[:, t, :],
                        lhsT=ap[c][:, g, t, :].bitcast(E2M1),
                        lhsT_scale=asp[c][:, g, t, :],
                        rhs=xc[u][:, i, g, :].bitcast(E4M3),
                        rhs_scale=xs[u][:, i, g, :],
                        start=(g == 0),
                        stop=(g == 1),
                    )
            hb[(u, i)] = h

        def mult(u, i):
            c, j0, n = units[u]
            if u not in yg:
                yg[u] = work.tile([128, n, 128, 4], BF16, name="yg%d" % n, align_bytes=64, bufs=4 if n == 2 else 2)
            nc.vector.tensor_tensor(
                out=yg[u][:, i, :, :].rearrange("p (b e) t -> p b t e", e=4),
                in0=hb[(u, i)][:].rearrange("p t (b e) -> p b t e", e=4),
                in1=sig[c][:, :, j0 + i, :].rearrange("p t (b e) -> p b t e", e=4),
                op=ALU.mult,
            )

        def qy(u):
            n = units[u][2]
            yc[u] = work.tile([128, n, 128], U32, name="yc%d" % n, align_bytes=64, bufs=4)
            ys[u] = work.tile([128, n, 128], U8, name="ys%d" % n, align_bytes=64, bufs=4)
            nc.vector.quantize_mx(
                out=yc[u][:].rearrange("p i n -> p (i n)").bitcast(E4M3),
                scales=ys[u][:].rearrange("p i n -> p (i n)"),
                in_=yg[u][:].rearrange("p i n k -> p (i n k)"),
            )

        def mm2(u, i):
            c = units[u][0]
            o = op.tile([128, 512], F32, name="o")
            nc.tensor.matmul_mx(
                out=o[:],
                lhsT=yc[u][:, i, :].bitcast(E4M3),
                lhsT_scale=ys[u][:, i, :],
                rhs=qw[c][:].bitcast(E2M1),
                rhs_scale=qs[:, c, :],
                start=True,
                stop=True,
            )
            ob[(u, i)] = o

        o_sb = {}

        def outcopy(u, i, eng):
            c, j0, n = units[u]
            if u not in o_sb:
                o_sb[u] = work.tile([128, n, 512], F32, name="ot%d" % n, bufs=4)
            if eng == "s":
                nc.scalar.copy(out=o_sb[u][:, i, :], in_=ob[(u, i)][:])
            else:
                nc.vector.tensor_copy(out=o_sb[u][:, i, :], in_=ob[(u, i)][:])
            if i == n - 1:
                nc.sync.dma_start(
                    out=out[c].rearrange("(j p) n -> p j n", j=J)[:, j0 : j0 + n, :],
                    in_=o_sb[u][:],
                )

        sig_work = {}
        first = {}
        step_of = [s for s, row in enumerate(steps) for u in row for i in range(units[u][2])]
        for s, row in enumerate(steps):
            for u in row:
                first.setdefault(units[u][0], s)
        sig_work.setdefault(0, []).extend([(0, t, 0, 1) for t in range(4)])
        sig_work.setdefault(1, []).extend([(0, t, 1, 1) for t in range(4)])
        sig_work.setdefault(2, []).extend([(0, t, 2, 2) for t in range(4)])
        sig_work.setdefault(3, []).extend([(0, t, 4, 4) for t in range(2)])
        sig_work.setdefault(4, []).extend([(0, t, 4, 4) for t in range(2, 4)])
        for c in range(1, G):
            for t in range(4):
                sig_work.setdefault(step_of[min(8 * c - (2 if c == 1 else SL) + 2 * t, 31)], []).append((c, t, 0, J))

        def tiles_of(s):
            if s < 0 or s >= len(steps):
                return []
            return [(u, i) for u in steps[s] for i in range(units[u][2])]

        perm_work = {0: [(perm_scales, (nc.vector, 0, g)) for g in range(2)]}
        for c in range(1, G):
            for g in range(2):
                perm_work.setdefault(step_of[8 * c - 2 * PL + 4 * g], []).append((perm_words, (nc.vector, c, g, 0, 4)))
                perm_work.setdefault(step_of[8 * c - 2 * PL + 4 * g + 2], []).append((perm_scales, (nc.vector, c, g)))
        loaded = 5
        ns = len(steps)
        count = 0
        for s in range(ns + L2):
            cur = tiles_of(s)
            mid = tiles_of(s - L1)
            last = tiles_of(s - L2)
            while loaded < len(units) and cur and loaded <= cur[-1][0] + 5:
                load_x(loaded)
                if loaded == 5:
                    load_lnu(1)
                c, j0, n = units[loaded]
                if j0 == 0 and c > 0:
                    load_q(c)
                    if c + 1 < G:
                        load_lnu(c + 1)
                if j0 == 4 and c + 1 < G and c + 1 > 1:
                    load_a(c + 1)
                loaded += 1

            def front():
                if s == 2:
                    spread(1)
                for u, i in cur:
                    transposes(u, i)

            def back():
                order = [(k, f) for k in range(4) for f in range(2)]
                if s == ns + L1 - 1:
                    order = [(k, f) for f in range(2) for k in range(4)]
                for k, f in order:
                    if f == 0 and k < len(mid):
                        mm1(*mid[k])
                        mult(*mid[k])
                    if f == 1 and k < len(last):
                        mm2(*last[k])
                        outcopy(last[k][0], last[k][1], "v" if s == ns + L2 - 1 and k == 0 else "s")

            qy_units = steps[s - L1 - 1] if 0 <= s - L1 - 1 < ns else []
            if s == ns:
                for u in qy_units:
                    qy(u)
            for u in (steps[s - 1] if 1 <= s <= ns else []):
                qx(u)
            if s != ns:
                for u in qy_units:
                    qy(u)
            if s == BF:
                back()
                front()
            else:
                front()
            for k, (u, i) in enumerate(cur):
                tout(u, i, "v" if VT[count % 2] != (s < 2) else "s")
                count += 1
            for args in sig_work.get(s, []):
                sigmoid(*args)
            for f, args in perm_work.get(s, []):
                f(*args)
            if s != BF:
                back()
